import numpy as np
import ml_dtypes


def mxq(x, axis, fmt="e4m3"):
    dtype, down = {"e4m3": (ml_dtypes.float8_e4m3fn, 7), "e5m2": (ml_dtypes.float8_e5m2, 14)}[fmt]
    v = np.moveaxis(np.asarray(x, np.float32).astype(ml_dtypes.bfloat16).astype(np.float64), axis, -1)
    blocks = v.reshape(v.shape[:-1] + (-1, 32))
    amax = np.abs(blocks).max(-1, keepdims=True)
    byte = np.maximum(np.where(amax > 0, np.frexp(amax)[1] - 1 + 127, 0) - down, 1)
    scale = np.exp2(byte - 127.0)
    codes = (blocks / scale).astype(np.float32).astype(dtype).astype(np.float64)
    return np.moveaxis((codes * scale).reshape(v.shape), -1, axis)


WIDE = False


def mx_kscale(k):
    if not WIDE:
        return np.ones(k)
    levels = np.array([10, -10, 5, -5, 0])
    if k % 512:
        return np.exp2(np.random.permutation(np.resize(levels, k // 32))).repeat(32)
    a = np.empty((k // 512, 16))
    for p in range(k // 512):
        a[p, :8] = np.random.permutation(np.resize(levels, 8))
        for g in range(8):
            far = levels[np.abs(levels - a[p, g]) >= 10]
            a[p, g + 8] = far[np.random.randint(len(far))]
    return np.exp2(a.ravel()).repeat(32)


def f64(x):
    return np.asarray(x).astype(np.float64)


def striped8(idx):
    return np.asarray(idx).reshape(8, -1, 16).transpose(0, 2, 1).reshape(128, -1).astype(np.uint16)


def unstriped8(offs):
    return offs.reshape(8, 16, -1).transpose(0, 2, 1).reshape(8, -1).astype(np.int64)


def pick8(x, idx, run):
    r = np.arange(len(x))
    return x[r[:, None], idx[r % (8 * run) // run]]


E2M1 = np.array([0.0, 0.5, 1.0, 1.5, 2.0, 3.0, 4.0, 6.0, -0.0, -0.5, -1.0, -1.5, -2.0, -3.0, -4.0, -6.0])


def pack_weight(w, fmt):
    k, n = w.shape
    w = f64(np.asarray(w, np.float32).astype(ml_dtypes.bfloat16)).reshape(k // 32, 32, n)
    amax = np.abs(w).max(1)
    if fmt == "e4m3":
        byte = np.frexp(amax)[1] - 1 + 127 - 7
    else:
        mant, ex = np.frexp(amax / 6.0)
        byte = np.where(mant > 0.5, ex, ex - 1) + 127
    byte = np.clip(np.where(amax > 0, byte, 1), 1, 254)
    scaled = (w * np.exp2(127.0 - byte)[:, None, :]).reshape(k, n).astype(np.float32)
    by_word = np.ascontiguousarray(scaled.reshape(k // 512, 128, 4, n).transpose(0, 1, 3, 2))
    if fmt == "e4m3":
        words = by_word.astype(ml_dtypes.float8_e4m3fn).view(np.uint8)
    else:
        c = by_word.astype(ml_dtypes.float4_e2m1fn).view(np.uint8) & 0xF
        words = (c[..., 0::2] | (c[..., 1::2] << 4)).reshape(k // 512, 128, 2 * n)
    return np.ascontiguousarray(words), np.ascontiguousarray(byte.astype(np.uint8).reshape(k // 512, 16, n))


def unpack_weight(words, scales, fmt):
    g, _, n = scales.shape
    words = np.ascontiguousarray(words).reshape(g, 128, n, -1)
    if fmt == "e4m3":
        vals = words.view(ml_dtypes.float8_e4m3fn).astype(np.float64)
    else:
        nib = np.empty((g, 128, n, 4), np.uint8)
        nib[..., 0::2] = words & 0xF
        nib[..., 1::2] = words >> 4
        vals = E2M1[nib]
    vals = vals * np.repeat(np.exp2(scales.astype(np.float64) - 127.0), 8, axis=1)[..., None]
    return vals.transpose(0, 1, 3, 2).reshape(g * 512, n)


D, T, U, I, Q = 512, 1024, 1024, 512, 128


def setup_inputs():
    n = np.random.standard_normal
    idx = np.stack([np.random.permutation(T)[:I] for _ in range(8)])
    idx2 = np.stack([np.random.permutation(U)[:I] for _ in range(8)])
    idx3 = np.stack([np.random.permutation(U)[:I] for _ in range(8)])
    idx4 = np.stack([np.random.permutation(U)[:I] for _ in range(8)])
    idx5 = np.stack([np.random.permutation(T)[:I] for _ in range(8)])
    fd = mx_kscale(D)
    keysp = pack_weight(n((D, T)) / fd[:, None], "e2m1")
    notesp = pack_weight(n((D, U)) / fd[:, None], "e4m3")
    return {
        "query": (n((D, Q)) * 1.0 / np.sqrt(D) * fd[:, None]).astype(np.float32),
        "keys_words": keysp[0],
        "keys_scales": keysp[1],
        "notes_words": notesp[0],
        "notes_scales": notesp[1],
        "offs": striped8(idx),
        "offs2": striped8(idx2),
        "offs3": striped8(idx3),
        "offs4": striped8(idx4),
        "offs5": striped8(idx5),
    }


def reference(query, keys_words, keys_scales, notes_words, notes_scales, offs, offs2, offs3, offs4, offs5):
    idx = unstriped8(offs)
    idx2 = unstriped8(offs2)
    idx3 = unstriped8(offs3)
    idx4 = unstriped8(offs4)
    idx5 = unstriped8(offs5)
    keysu = unpack_weight(keys_words, keys_scales, "e2m1")
    notesu = unpack_weight(notes_words, notes_scales, "e4m3")
    queryq = mxq(f64(query), 0, "e4m3")
    a = queryq.T @ keysu
    b = queryq.T @ notesu
    w = pick8(a, idx, 16) * 1.25
    w1 = np.pad(w, ((0, 0), (1, 0)))[:, :I]
    r = np.maximum(w1, pick8(b, idx2, 16))
    f1 = np.zeros((Q, U))
    f1[np.arange(Q)[:, None], idx3[np.arange(Q) % 128 // 16]] = r
    bb = b - f1
    v = pick8(bb, idx4, 16) + w
    y = np.minimum(v, pick8(a, idx5, 16))
    return y

@@ -1,0 +1,138 @@
+from contextlib import ExitStack
+
+import concourse.mybir as mybir
+
+D, T, U, SLOTS, Q = 512, 1024, 1024, 512, 128
+FLOPS = 2 * D * Q * (T + U)
+
+F32 = mybir.dt.float32
+BF16 = mybir.dt.bfloat16
+I32 = mybir.dt.int32
+U32 = mybir.dt.uint32
+U16 = mybir.dt.uint16
+U8 = mybir.dt.uint8
+FP8X4 = mybir.dt.float8_e4m3fn_x4
+FP4X4 = mybir.dt.float4_e2m1fn_x4
+ALU = mybir.AluOpType
+COPY = mybir.ActivationFunctionType.Copy
+
+P = 128
+PAD = 8
+
+
+def cols(lo, hi):
+    return slice(lo // 16, hi // 16)
+
+
+def tile_attend_ringpass_two_kernel(tc, query, keys_words, keys_scales, notes_words, notes_scales,
+                                     offs, offs2, offs3, offs4, offs5, out):
+    nc = tc.nc
+    with ExitStack() as ctx:
+        sb = ctx.enter_context(tc.tile_pool(name="sb", bufs=1))
+        ps = ctx.enter_context(tc.psum_pool(name="ps", bufs=1))
+
+        k_plane = sb.tile([P, T], U8, align_bytes=64)
+        n_plane = sb.tile([P, U], U8, align_bytes=64)
+        nc.vector.memset(k_plane[:].bitcast(I32), 0)
+        nc.vector.memset(n_plane[:].bitcast(I32), 0)
+
+        def load_scales(queue, plane, scales, g):
+            queue.dma_start(out=plane[32 * g : 32 * g + 4, :].bitcast(I32),
+                            in_=scales[0, 4 * g : 4 * g + 4, :].bitcast(I32))
+
+        q_raw = sb.tile([P, 4, Q], F32)
+        k_words = sb.tile([P, 2 * T], U8, align_bytes=64)
+        n_words = sb.tile([P, U], U32, align_bytes=64)
+        l1 = sb.tile([P, SLOTS // 16], U16)
+        l2 = sb.tile([P, SLOTS // 16], U16)
+        l3 = sb.tile([P, SLOTS // 16], U16)
+        l4 = sb.tile([P, SLOTS // 16], U16)
+        l5 = sb.tile([P, SLOTS // 16], U16)
+        nc.sync.dma_start(out=q_raw[:], in_=query.rearrange("(p j) q -> p j q", j=4))
+        for g in range(4):
+            load_scales(nc.sync if g % 2 else nc.scalar, k_plane, keys_scales, g)
+        load_scales(nc.scalar, n_plane, notes_scales, 0)
+        nc.sync.dma_start(out=k_words[:].bitcast(I32), in_=keys_words[0].bitcast(I32))
+        nc.sync.dma_start(out=n_words[:].bitcast(I32),
+                          in_=notes_words[0].rearrange("p n t -> p (n t)").bitcast(I32))
+        nc.sync.dma_start(l1[:], offs)
+        for g in range(1, 4):
+            load_scales(nc.sync, n_plane, notes_scales, g)
+        nc.sync.dma_start(l2[:], offs2)
+        nc.sync.dma_start(l3[:], offs3)
+        nc.sync.dma_start(l5[:], offs5)
+        nc.sync.dma_start(l4[:], offs4)
+
+        f1 = sb.tile([P, U], F32)
+        nc.vector.memset(f1[:], 0.0)
+        w_pad = sb.tile([P, PAD + SLOTS], F32)
+        nc.vector.memset(w_pad[:, PAD - 1 : PAD], 0.0)
+
+        q_bf = sb.tile([P, Q, 4], BF16, align_bytes=64)
+        nc.vector.tensor_copy(out=q_bf[:].rearrange("p (c i) t -> p c t i", i=4),
+                              in_=q_raw[:].rearrange("p t (c i) -> p c t i", i=4))
+        q_codes = sb.tile([P, Q], U32, align_bytes=64)
+        q_plane = sb.tile([P, Q], U8, align_bytes=64)
+        nc.vector.quantize_mx(out=q_codes[:].bitcast(FP8X4), scales=q_plane[:],
+                              in_=q_bf[:].rearrange("p q t -> p (q t)"))
+
+        def score_notes(name, lo, hi):
+            bank = ps.tile([P, hi - lo], F32, name=name)
+            nc.tensor.matmul_mx(out=bank[:], lhsT=q_codes[:].bitcast(FP8X4), lhsT_scale=q_plane[:],
+                                rhs=n_words[:, lo:hi].bitcast(FP8X4), rhs_scale=n_plane[:, lo:hi],
+                                start=True, stop=True)
+            return bank
+
+        def score_keys(name, lo, hi):
+            bank = ps.tile([P, hi - lo], F32, name=name)
+            nc.tensor.matmul_mx(out=bank[:], lhsT=q_codes[:].bitcast(FP8X4), lhsT_scale=q_plane[:],
+                                rhs=k_words[:, 2 * lo : 2 * hi].bitcast(FP4X4), rhs_scale=k_plane[:, lo:hi],
+                                start=True, stop=True)
+            return bank
+
+        a0 = score_keys("a0", 0, 512)
+        a1 = score_keys("a1", 512, 768)
+        a2 = score_keys("a2", 768, 1024)
+        b0 = score_notes("b0", 0, 512)
+        b1 = score_notes("b1", 512, 768)
+        b2 = score_notes("b2", 768, 1024)
+
+        a = sb.tile([P, T], F32)
+        b = sb.tile([P, U], F32)
+        g2 = sb.tile([P, SLOTS], F32)
+        g5 = sb.tile([P, SLOTS], F32)
+        r = sb.tile([P, SLOTS], F32)
+        nc.scalar.activation(a[:, 0:512], a0[:], COPY)
+        nc.vector.tensor_copy(a[:, 512:768], a1[:])
+        nc.vector.tensor_copy(a[:, 768:1024], a2[:])
+
+        nc.vector.tensor_scalar(w_pad[:, PAD : PAD + 256], a[:].indirect(l1[:, cols(0, 256)]), 1.25, 0.0,
+                                op0=ALU.mult, op1=ALU.add)
+        nc.scalar.activation(w_pad[:, PAD + 256 : PAD + 512], a[:].indirect(l1[:, cols(256, 512)]), COPY, scale=1.25)
+
+        nc.scalar.activation(b[:, 0:512], b0[:], COPY)
+        nc.vector.tensor_copy(b[:, 512:768], b1[:])
+        nc.vector.tensor_copy(b[:, 768:1024], b2[:])
+
+        nc.vector.tensor_copy(g2[:, 0:256], b[:].indirect(l2[:, cols(0, 256)]))
+        nc.scalar.activation(g2[:, 256:512], b[:].indirect(l2[:, cols(256, 512)]), COPY)
+        nc.scalar.activation(g5[:], a[:].indirect(l5[:]), COPY)
+
+        for lo, hi in ((0, 256), (256, 512)):
+            nc.vector.tensor_tensor(r[:, lo:hi], w_pad[:, PAD - 1 + lo : PAD - 1 + hi], g2[:, lo:hi], ALU.max)
+        for lo, hi in ((0, 256), (256, 512)):
+            nc.vector.tensor_copy(f1[:].indirect(l3[:, cols(lo, hi)]), r[:, lo:hi])
+
+        bb = sb.tile([P, U], F32)
+        nc.vector.tensor_tensor(bb[:], b[:], f1[:], ALU.subtract)
+
+        v = sb.tile([P, SLOTS], F32)
+        g4 = sb.tile([P, 256], F32)
+        y = sb.tile([P, SLOTS], F32)
+        nc.scalar.activation(g4[:], bb[:].indirect(l4[:, cols(256, 512)]), COPY)
+        nc.vector.tensor_tensor(v[:, 0:256], bb[:].indirect(l4[:, cols(0, 256)]), w_pad[:, PAD : PAD + 256], ALU.add)
+        nc.vector.tensor_tensor(v[:, 256:512], g4[:], w_pad[:, PAD + 256 : PAD + 512], ALU.add)
+        nc.vector.tensor_tensor(y[:, 0:256], v[:, 0:256], g5[:, 0:256], ALU.min)
+        nc.sync.dma_start(out=out[:, 0:256], in_=y[:, 0:256])
+        nc.vector.tensor_tensor(y[:, 256:512], v[:, 256:512], g5[:, 256:512], ALU.min)
+        nc.scalar.dma_start(out=out[:, 256:512], in_=y[:, 256:512])

@@ -126,13 +126,14 @@ def tile_attend_ringpass_two_kernel(tc, query, keys_words, keys_scales, notes_wo
         bb = sb.tile([P, U], F32)
         nc.vector.tensor_tensor(bb[:], b[:], f1[:], ALU.subtract)
 
+        g4 = sb.tile([P, SLOTS], F32)
         v = sb.tile([P, SLOTS], F32)
-        g4 = sb.tile([P, 256], F32)
         y = sb.tile([P, SLOTS], F32)
-        nc.scalar.activation(g4[:], bb[:].indirect(l4[:, cols(256, 512)]), COPY)
-        nc.vector.tensor_tensor(v[:, 0:256], bb[:].indirect(l4[:, cols(0, 256)]), w_pad[:, PAD : PAD + 256], ALU.add)
-        nc.vector.tensor_tensor(v[:, 256:512], g4[:], w_pad[:, PAD + 256 : PAD + 512], ALU.add)
-        nc.vector.tensor_tensor(y[:, 0:256], v[:, 0:256], g5[:, 0:256], ALU.min)
-        nc.sync.dma_start(out=out[:, 0:256], in_=y[:, 0:256])
-        nc.vector.tensor_tensor(y[:, 256:512], v[:, 256:512], g5[:, 256:512], ALU.min)
-        nc.scalar.dma_start(out=out[:, 256:512], in_=y[:, 256:512])
+        nc.vector.tensor_copy(g4[:, 0:256], bb[:].indirect(l4[:, cols(0, 256)]))
+        nc.scalar.activation(g4[:, 256:512], bb[:].indirect(l4[:, cols(256, 512)]), COPY)
+        for lo, hi in ((0, 256), (256, 512)):
+            nc.vector.tensor_tensor(v[:, lo:hi], g4[:, lo:hi], w_pad[:, PAD + lo : PAD + hi], ALU.add)
+        for c in range(4):
+            lo, hi = 128 * c, 128 * (c + 1)
+            nc.vector.tensor_tensor(y[:, lo:hi], v[:, lo:hi], g5[:, lo:hi], ALU.min)
+            (nc.scalar if c % 2 else nc.sync).dma_start(out=out[:, lo:hi], in_=y[:, lo:hi])

from contextlib import ExitStack

import concourse.mybir as mybir

D, T, U, SLOTS, Q = 512, 1024, 1024, 512, 128
FLOPS = 2 * D * Q * (T + U)

F32 = mybir.dt.float32
BF16 = mybir.dt.bfloat16
I32 = mybir.dt.int32
U32 = mybir.dt.uint32
U16 = mybir.dt.uint16
U8 = mybir.dt.uint8
FP8X4 = mybir.dt.float8_e4m3fn_x4
FP4X4 = mybir.dt.float4_e2m1fn_x4
ALU = mybir.AluOpType
COPY = mybir.ActivationFunctionType.Copy

P = 128
PAD = 8


def cols(lo, hi):
    return slice(lo // 16, hi // 16)


def tile_attend_ringpass_two_kernel(tc, query, keys_words, keys_scales, notes_words, notes_scales,
                                     offs, offs2, offs3, offs4, offs5, out):
    nc = tc.nc
    with ExitStack() as ctx:
        sb = ctx.enter_context(tc.tile_pool(name="sb", bufs=1))
        ps = ctx.enter_context(tc.psum_pool(name="ps", bufs=1))

        k_plane = sb.tile([P, T], U8, align_bytes=64)
        n_plane = sb.tile([P, U], U8, align_bytes=64)
        nc.vector.memset(k_plane[:].bitcast(I32), 0)
        nc.vector.memset(n_plane[:].bitcast(I32), 0)

        def load_scales(queue, plane, scales, g):
            queue.dma_start(out=plane[32 * g : 32 * g + 4, :].bitcast(I32),
                            in_=scales[0, 4 * g : 4 * g + 4, :].bitcast(I32))

        q_raw = sb.tile([P, 4, Q], F32)
        k_words = sb.tile([P, 2 * T], U8, align_bytes=64)
        n_words = sb.tile([P, U], U32, align_bytes=64)
        l1 = sb.tile([P, SLOTS // 16], U16)
        l2 = sb.tile([P, SLOTS // 16], U16)
        l3 = sb.tile([P, SLOTS // 16], U16)
        l4 = sb.tile([P, SLOTS // 16], U16)
        l5 = sb.tile([P, SLOTS // 16], U16)
        nc.sync.dma_start(out=q_raw[:], in_=query.rearrange("(p j) q -> p j q", j=4))
        for g in range(4):
            load_scales(nc.sync if g % 2 else nc.scalar, k_plane, keys_scales, g)
        load_scales(nc.scalar, n_plane, notes_scales, 0)
        nc.sync.dma_start(out=k_words[:].bitcast(I32), in_=keys_words[0].bitcast(I32))
        nc.sync.dma_start(out=n_words[:].bitcast(I32),
                          in_=notes_words[0].rearrange("p n t -> p (n t)").bitcast(I32))
        nc.sync.dma_start(l1[:], offs)
        for g in range(1, 4):
            load_scales(nc.sync, n_plane, notes_scales, g)
        nc.sync.dma_start(l2[:], offs2)
        nc.sync.dma_start(l3[:], offs3)
        nc.sync.dma_start(l5[:], offs5)
        nc.sync.dma_start(l4[:], offs4)

        f1 = sb.tile([P, U], F32)
        nc.vector.memset(f1[:], 0.0)
        w_pad = sb.tile([P, PAD + SLOTS], F32)
        nc.vector.memset(w_pad[:, PAD - 1 : PAD], 0.0)

        q_bf = sb.tile([P, Q, 4], BF16, align_bytes=64)
        nc.vector.tensor_copy(out=q_bf[:].rearrange("p (c i) t -> p c t i", i=4),
                              in_=q_raw[:].rearrange("p t (c i) -> p c t i", i=4))
        q_codes = sb.tile([P, Q], U32, align_bytes=64)
        q_plane = sb.tile([P, Q], U8, align_bytes=64)
        nc.vector.quantize_mx(out=q_codes[:].bitcast(FP8X4), scales=q_plane[:],
                              in_=q_bf[:].rearrange("p q t -> p (q t)"))

        def score_notes(name, lo, hi):
            bank = ps.tile([P, hi - lo], F32, name=name)
            nc.tensor.matmul_mx(out=bank[:], lhsT=q_codes[:].bitcast(FP8X4), lhsT_scale=q_plane[:],
                                rhs=n_words[:, lo:hi].bitcast(FP8X4), rhs_scale=n_plane[:, lo:hi],
                                start=True, stop=True)
            return bank

        def score_keys(name, lo, hi):
            bank = ps.tile([P, hi - lo], F32, name=name)
            nc.tensor.matmul_mx(out=bank[:], lhsT=q_codes[:].bitcast(FP8X4), lhsT_scale=q_plane[:],
                                rhs=k_words[:, 2 * lo : 2 * hi].bitcast(FP4X4), rhs_scale=k_plane[:, lo:hi],
                                start=True, stop=True)
            return bank

        a0 = score_keys("a0", 0, 512)
        a1 = score_keys("a1", 512, 768)
        a2 = score_keys("a2", 768, 1024)
        b0 = score_notes("b0", 0, 512)
        b1 = score_notes("b1", 512, 768)
        b2 = score_notes("b2", 768, 1024)

        a = sb.tile([P, T], F32)
        b = sb.tile([P, U], F32)
        g2 = sb.tile([P, SLOTS], F32)
        g5 = sb.tile([P, SLOTS], F32)
        r = sb.tile([P, SLOTS], F32)
        nc.scalar.activation(a[:, 0:512], a0[:], COPY)
        nc.vector.tensor_copy(a[:, 512:768], a1[:])
        nc.vector.tensor_copy(a[:, 768:1024], a2[:])

        nc.vector.tensor_scalar(w_pad[:, PAD : PAD + 256], a[:].indirect(l1[:, cols(0, 256)]), 1.25, 0.0,
                                op0=ALU.mult, op1=ALU.add)
        nc.scalar.activation(w_pad[:, PAD + 256 : PAD + 512], a[:].indirect(l1[:, cols(256, 512)]), COPY, scale=1.25)

        nc.scalar.activation(b[:, 0:512], b0[:], COPY)
        nc.vector.tensor_copy(b[:, 512:768], b1[:])
        nc.vector.tensor_copy(b[:, 768:1024], b2[:])

        nc.vector.tensor_copy(g2[:, 0:256], b[:].indirect(l2[:, cols(0, 256)]))
        nc.scalar.activation(g2[:, 256:512], b[:].indirect(l2[:, cols(256, 512)]), COPY)
        nc.scalar.activation(g5[:], a[:].indirect(l5[:]), COPY)

        for lo, hi in ((0, 256), (256, 512)):
            nc.vector.tensor_tensor(r[:, lo:hi], w_pad[:, PAD - 1 + lo : PAD - 1 + hi], g2[:, lo:hi], ALU.max)
        for lo, hi in ((0, 256), (256, 512)):
            nc.vector.tensor_copy(f1[:].indirect(l3[:, cols(lo, hi)]), r[:, lo:hi])

        bb = sb.tile([P, U], F32)
        nc.vector.tensor_tensor(bb[:], b[:], f1[:], ALU.subtract)

        g4 = sb.tile([P, SLOTS], F32)
        v = sb.tile([P, SLOTS], F32)
        y = sb.tile([P, SLOTS], F32)
        nc.vector.tensor_copy(g4[:, 0:256], bb[:].indirect(l4[:, cols(0, 256)]))
        nc.scalar.activation(g4[:, 256:512], bb[:].indirect(l4[:, cols(256, 512)]), COPY)
        for lo, hi in ((0, 256), (256, 512)):
            nc.vector.tensor_tensor(v[:, lo:hi], g4[:, lo:hi], w_pad[:, PAD + lo : PAD + hi], ALU.add)
        for c in range(4):
            lo, hi = 128 * c, 128 * (c + 1)
            nc.vector.tensor_tensor(y[:, lo:hi], v[:, lo:hi], g5[:, lo:hi], ALU.min)
            (nc.scalar if c % 2 else nc.sync).dma_start(out=out[:, lo:hi], in_=y[:, lo:hi])
